import numpy as np
import ml_dtypes

BF16 = ml_dtypes.bfloat16


def bf(x):
    return np.asarray(x, np.float32).astype(BF16)


def f32(x):
    return np.asarray(x, np.float32)


def f64(x):
    return np.asarray(x).astype(np.float64)


def striped(idx):
    return np.tile(idx.reshape(-1, 16).T, (8, 1))


S, K, H, M, N, D, V = 1024, 512, 128, 256, 512, 8, 64


def gelu_tanh(v):
    return 0.5 * v * (1.0 + np.tanh(np.sqrt(2.0 / np.pi) * (v + 0.044715 * v**3)))


def setup_inputs():
    return {"x": bf(np.random.standard_normal((K, S))), "w": bf(np.random.standard_normal((K, H)) / np.sqrt(K)), "b": f32(0.5 * np.random.standard_normal((H, 1))), "w2": bf(np.random.standard_normal((H, M)) / np.sqrt(H)), "offs": striped(np.random.permutation(S)[:N])}


def reference(x, w, b, w2, offs):
    idx = offs[:16].T.reshape(-1)
    t = gelu_tanh(f64(w).T @ f64(x) + f64(b))
    return (f64(w2).T @ t[:, idx]).reshape(M, V, D).max(axis=2)

@@ -1,0 +1,56 @@
+import concourse.mybir as mybir
+
+BF16, F32, U16 = mybir.dt.bfloat16, mybir.dt.float32, mybir.dt.uint16
+
+P = 128
+S, K, H, M, N, D, V = 1024, 512, 128, 256, 512, 8, 64
+KB = K // P
+BANK = 512
+PIECE = 256
+FLOPS = 2 * K * H * S + 2 * H * M * N
+
+
+def tile_rows_gcn2_gelu_max_kernel(tc, x, w, b, w2, offs, out):
+    nc = tc.nc
+    with (
+        tc.tile_pool(name="held", bufs=1) as held,
+        tc.psum_pool(name="psum", bufs=1) as psum,
+    ):
+        x_rows = x.rearrange("(p a) s -> p a s", a=KB)
+        w_sb = held.tile([P, KB, H], BF16, name="w_sb")
+        nc.scalar.dma_start(w_sb[:], w.rearrange("(p a) h -> p a h", a=KB))
+        bias = held.tile([P, 1], F32, name="bias")
+        nc.scalar.dma_start(bias[:], b)
+
+        x_whole = [held.tile([P, S], BF16, name=f"x_whole{a}") for a in range(2)]
+        for a in range(2):
+            nc.sync.dma_start(x_whole[a][:], x_rows[:, a, :])
+        x_half = [held.tile([P, 2, BANK], BF16, name=f"x_half{c}") for c in range(2)]
+        for c in range(2):
+            nc.sync.dma_start(x_half[c][:], x_rows[:, 2:4, c * BANK:(c + 1) * BANK])
+        w2_sb = held.tile([P, M], BF16, name="w2_sb")
+        nc.sync.dma_start(w2_sb[:], w2)
+        offsets = held.tile([P, N // 16], U16, name="offsets")
+        nc.sync.dma_start(offsets[:], offs)
+
+        h = held.tile([P, S], BF16, name="h")
+        for c in range(2):
+            cols = slice(c * BANK, (c + 1) * BANK)
+            pre = psum.tile([P, BANK], F32, name=f"pre{c}")
+            for a in range(KB):
+                moving = x_whole[a][:, cols] if a < 2 else x_half[c][:, a - 2, :]
+                nc.tensor.matmul(pre[:], w_sb[:, a, :], moving, start=(a == 0), stop=(a == KB - 1))
+            nc.scalar.activation(h[:, cols], pre[:], mybir.ActivationFunctionType.Gelu_apprx_tanh,
+                                 bias=bias[:])
+
+        nodes = PIECE // D
+        for mb in range(M // P):
+            pooled = held.tile([P, V], F32, name=f"pooled{mb}")
+            for q in range(N // PIECE):
+                prod = psum.tile([P, PIECE], F32, name=f"prod{mb}_{q}")
+                picked = h[:].indirect(offsets[:, q * PIECE // 16:(q + 1) * PIECE // 16])
+                nc.tensor.matmul(prod[:], w2_sb[:, mb * P:(mb + 1) * P], picked, start=True, stop=True)
+                nc.vector.tensor_reduce(pooled[:, q * nodes:(q + 1) * nodes],
+                                        prod[:].rearrange("p (v d) -> p v d", d=D),
+                                        mybir.AxisListType.X, mybir.AluOpType.max)
+            nc.sync.dma_start(out[mb * P:(mb + 1) * P, :], pooled[:])

@@ -7,6 +7,7 @@ S, K, H, M, N, D, V = 1024, 512, 128, 256, 512, 8, 64
 KB = K // P
 BANK = 512
 PIECE = 256
+WARM_COLS = 32
 FLOPS = 2 * K * H * S + 2 * H * M * N
 
 
@@ -32,6 +33,13 @@ def tile_rows_gcn2_gelu_max_kernel(tc, x, w, b, w2, offs, out):
         nc.sync.dma_start(w2_sb[:], w2)
         offsets = held.tile([P, N // 16], U16, name="offsets")
         nc.sync.dma_start(offsets[:], offs)
+
+        zeros = held.tile([P, WARM_COLS], BF16, name="zeros")
+        nc.gpsimd.memset(zeros[:], 0.0)
+        warm = psum.tile([WARM_COLS, BANK], F32, name="warm")
+        for i in range(4):
+            nc.tensor.matmul(warm[:], zeros[:], zeros[:, 0:1].to_broadcast([P, BANK]),
+                             start=True, stop=True)
 
         h = held.tile([P, S], BF16, name="h")
         for c in range(2):

import concourse.mybir as mybir

BF16, F32, U16 = mybir.dt.bfloat16, mybir.dt.float32, mybir.dt.uint16

P = 128
S, K, H, M, N, D, V = 1024, 512, 128, 256, 512, 8, 64
KB = K // P
BANK = 512
PIECE = 256
WARM_COLS = 32
FLOPS = 2 * K * H * S + 2 * H * M * N


def tile_rows_gcn2_gelu_max_kernel(tc, x, w, b, w2, offs, out):
    nc = tc.nc
    with (
        tc.tile_pool(name="held", bufs=1) as held,
        tc.psum_pool(name="psum", bufs=1) as psum,
    ):
        x_rows = x.rearrange("(p a) s -> p a s", a=KB)
        w_sb = held.tile([P, KB, H], BF16, name="w_sb")
        nc.scalar.dma_start(w_sb[:], w.rearrange("(p a) h -> p a h", a=KB))
        bias = held.tile([P, 1], F32, name="bias")
        nc.scalar.dma_start(bias[:], b)

        x_whole = [held.tile([P, S], BF16, name=f"x_whole{a}") for a in range(2)]
        for a in range(2):
            nc.sync.dma_start(x_whole[a][:], x_rows[:, a, :])
        x_half = [held.tile([P, 2, BANK], BF16, name=f"x_half{c}") for c in range(2)]
        for c in range(2):
            nc.sync.dma_start(x_half[c][:], x_rows[:, 2:4, c * BANK:(c + 1) * BANK])
        w2_sb = held.tile([P, M], BF16, name="w2_sb")
        nc.sync.dma_start(w2_sb[:], w2)
        offsets = held.tile([P, N // 16], U16, name="offsets")
        nc.sync.dma_start(offsets[:], offs)

        zeros = held.tile([P, WARM_COLS], BF16, name="zeros")
        nc.gpsimd.memset(zeros[:], 0.0)
        warm = psum.tile([WARM_COLS, BANK], F32, name="warm")
        for i in range(4):
            nc.tensor.matmul(warm[:], zeros[:], zeros[:, 0:1].to_broadcast([P, BANK]),
                             start=True, stop=True)

        h = held.tile([P, S], BF16, name="h")
        for c in range(2):
            cols = slice(c * BANK, (c + 1) * BANK)
            pre = psum.tile([P, BANK], F32, name=f"pre{c}")
            for a in range(KB):
                moving = x_whole[a][:, cols] if a < 2 else x_half[c][:, a - 2, :]
                nc.tensor.matmul(pre[:], w_sb[:, a, :], moving, start=(a == 0), stop=(a == KB - 1))
            nc.scalar.activation(h[:, cols], pre[:], mybir.ActivationFunctionType.Gelu_apprx_tanh,
                                 bias=bias[:])

        nodes = PIECE // D
        for mb in range(M // P):
            pooled = held.tile([P, V], F32, name=f"pooled{mb}")
            for q in range(N // PIECE):
                prod = psum.tile([P, PIECE], F32, name=f"prod{mb}_{q}")
                picked = h[:].indirect(offsets[:, q * PIECE // 16:(q + 1) * PIECE // 16])
                nc.tensor.matmul(prod[:], w2_sb[:, mb * P:(mb + 1) * P], picked, start=True, stop=True)
                nc.vector.tensor_reduce(pooled[:, q * nodes:(q + 1) * nodes],
                                        prod[:].rearrange("p (v d) -> p v d", d=D),
                                        mybir.AxisListType.X, mybir.AluOpType.max)
            nc.sync.dma_start(out[mb * P:(mb + 1) * P, :], pooled[:])
